import numpy as np
import ml_dtypes


def mxq(x, axis, fmt="e4m3"):
    dtype, down = {"e4m3": (ml_dtypes.float8_e4m3fn, 7), "e5m2": (ml_dtypes.float8_e5m2, 14)}[fmt]
    v = np.moveaxis(np.asarray(x, np.float32).astype(ml_dtypes.bfloat16).astype(np.float64), axis, -1)
    blocks = v.reshape(v.shape[:-1] + (-1, 32))
    amax = np.abs(blocks).max(-1, keepdims=True)
    byte = np.maximum(np.where(amax > 0, np.frexp(amax)[1] - 1 + 127, 0) - down, 1)
    scale = np.exp2(byte - 127.0)
    codes = (blocks / scale).astype(np.float32).astype(dtype).astype(np.float64)
    return np.moveaxis((codes * scale).reshape(v.shape), -1, axis)


WIDE = False


def mx_kscale(k):
    if not WIDE:
        return np.ones(k)
    levels = np.array([10, -10, 5, -5, 0])
    if k % 512:
        return np.exp2(np.random.permutation(np.resize(levels, k // 32))).repeat(32)
    a = np.empty((k // 512, 16))
    for p in range(k // 512):
        a[p, :8] = np.random.permutation(np.resize(levels, 8))
        for g in range(8):
            far = levels[np.abs(levels - a[p, g]) >= 10]
            a[p, g + 8] = far[np.random.randint(len(far))]
    return np.exp2(a.ravel()).repeat(32)


def f64(x):
    return np.asarray(x).astype(np.float64)


def striped(idx):
    return np.tile(np.asarray(idx).reshape(-1, 16).T, (8, 1)).astype(np.uint16)


def unstriped(offs):
    return offs[:16].T.reshape(-1).astype(np.int64)


E2M1 = np.array([0.0, 0.5, 1.0, 1.5, 2.0, 3.0, 4.0, 6.0, -0.0, -0.5, -1.0, -1.5, -2.0, -3.0, -4.0, -6.0])


def pack_weight(w, fmt):
    k, n = w.shape
    w = f64(np.asarray(w, np.float32).astype(ml_dtypes.bfloat16)).reshape(k // 32, 32, n)
    amax = np.abs(w).max(1)
    if fmt == "e4m3":
        byte = np.frexp(amax)[1] - 1 + 127 - 7
    else:
        mant, ex = np.frexp(amax / 6.0)
        byte = np.where(mant > 0.5, ex, ex - 1) + 127
    byte = np.clip(np.where(amax > 0, byte, 1), 1, 254)
    scaled = (w * np.exp2(127.0 - byte)[:, None, :]).reshape(k, n).astype(np.float32)
    by_word = np.ascontiguousarray(scaled.reshape(k // 512, 128, 4, n).transpose(0, 1, 3, 2))
    if fmt == "e4m3":
        words = by_word.astype(ml_dtypes.float8_e4m3fn).view(np.uint8)
    else:
        c = by_word.astype(ml_dtypes.float4_e2m1fn).view(np.uint8) & 0xF
        words = (c[..., 0::2] | (c[..., 1::2] << 4)).reshape(k // 512, 128, 2 * n)
    return np.ascontiguousarray(words), np.ascontiguousarray(byte.astype(np.uint8).reshape(k // 512, 16, n))


def unpack_weight(words, scales, fmt):
    g, _, n = scales.shape
    words = np.ascontiguousarray(words).reshape(g, 128, n, -1)
    if fmt == "e4m3":
        vals = words.view(ml_dtypes.float8_e4m3fn).astype(np.float64)
    else:
        nib = np.empty((g, 128, n, 4), np.uint8)
        nib[..., 0::2] = words & 0xF
        nib[..., 1::2] = words >> 4
        vals = E2M1[nib]
    vals = vals * np.repeat(np.exp2(scales.astype(np.float64) - 127.0), 8, axis=1)[..., None]
    return vals.transpose(0, 1, 3, 2).reshape(g * 512, n)


def sigmoid(v):
    return 1.0 / (1.0 + np.exp(-v))


D, T, I, Q, E, U, M = 512, 2048, 512, 256, 512, 1024, 1024


def setup_inputs():
    n = np.random.standard_normal
    idx = np.random.permutation(T)[:I]
    idx2 = np.random.permutation(U)[:I]
    idx3 = np.random.permutation(M)[:Q]
    fd = mx_kscale(D)
    fi = mx_kscale(I)
    ti = np.ones(T)
    ti[idx] = fi
    keysp = pack_weight(n((D, T)) / fd[:, None], "e4m3")
    return {
        "query": (n((D, Q)) * 0.7 / np.sqrt(D) * fd[:, None]).astype(np.float32),
        "query2": (n((D, Q)) * 0.7 / np.sqrt(D) * fd[:, None]).astype(np.float32),
        "keys_words": keysp[0],
        "keys_scales": keysp[1],
        "notes": (n((D, U)) / fd[:, None]).astype(np.float32),
        "os": (np.random.uniform(0.02, 0.08, (1, I)) * fi).astype(np.float32),
        "vals": (n((E, T)) / ti).astype(np.float32),
        "old": (n((E, M)) * 2.0).astype(np.float32),
        "fade": (np.random.uniform(0.3, 0.9, (1, M))).astype(np.float32),
        "offs": striped(idx),
        "offs2": striped(idx2),
        "offs3": striped(idx3),
    }


def reference(query, query2, keys_words, keys_scales, notes, os, vals, old, fade, offs, offs2, offs3):
    idx = unstriped(offs)
    idx2 = unstriped(offs2)
    idx3 = unstriped(offs3)
    keysu = unpack_weight(keys_words, keys_scales, "e4m3")
    queryq = mxq(f64(query), 0, "e4m3")
    keysidxg = keysu[:, idx]
    query2q = mxq(f64(query2), 0, "e4m3")
    notesidx2q = mxq(f64(notes)[:, idx2], 0, "e4m3")
    s = queryq.T @ keysidxg + query2q.T @ notesidx2q
    w = sigmoid(s)
    wo1 = w * f64(os)
    wt1 = wo1.T
    vt1 = f64(vals)[:, idx].T
    vt1q = mxq(vt1, 0, "e4m3")
    wt1q = mxq(wt1, 0, "e4m3")
    o = vt1q.T @ wt1q
    of = np.zeros((E, M))
    of[:, idx3] = o
    y = f64(old) * f64(fade) + of
    return y

@@ -1,0 +1,245 @@
+from contextlib import ExitStack
+
+import concourse.mybir as mybir
+from concourse.masks import make_identity
+
+D, T, I, Q, E, U, M = 512, 2048, 512, 256, 512, 1024, 1024
+FLOPS = 2 * (2 * D * Q * I + I * E * Q)
+
+F32 = mybir.dt.float32
+BF16 = mybir.dt.bfloat16
+I32 = mybir.dt.int32
+U32 = mybir.dt.uint32
+U16 = mybir.dt.uint16
+U8 = mybir.dt.uint8
+FP8X4 = mybir.dt.float8_e4m3fn_x4
+COPY = mybir.ActivationFunctionType.Copy
+SIGMOID = mybir.ActivationFunctionType.Sigmoid
+MULT = mybir.AluOpType.mult
+ADD = mybir.AluOpType.add
+
+P = 128
+PACK = 4
+BLOCKS = E // P
+HALF = Q // 2
+
+
+def tile_attend_twosources_written_lean_kernel(
+    tc, query, query2, keys_words, keys_scales, notes, slot_factor, vals, old, fade, offs, offs2, offs3, out
+):
+    nc = tc.nc
+    with ExitStack() as ctx:
+        lists = ctx.enter_context(tc.tile_pool(name="lists", bufs=1))
+        keep = ctx.enter_context(tc.tile_pool(name="keep", bufs=1))
+        psum = ctx.enter_context(tc.psum_pool(name="psum", bufs=1))
+
+        token_list = lists.tile([P, I // 16], U16, name="token_list")
+        note_list = lists.tile([P, I // 16], U16, name="note_list")
+        place_list = lists.tile([P, Q // 16], U16, name="place_list")
+
+        def held(name, shape, dtype, reuse=None):
+            return keep.tile(shape, dtype, name=name, tag=reuse or name, align_bytes=64)
+
+        key_bytes = held("key_bytes", [P, T], U8)
+        nc.vector.memset(key_bytes[:].bitcast(I32), 0)
+        factor = held("factor", [P, PACK], F32)
+        fade_cols = held("fade_cols", [P, 8], F32)
+        byte_rows = held("byte_rows", [4, 4, T // 4], I32)
+        windows = [held("window%d" % b, [P, M], F32) for b in range(BLOCKS)]
+        identity = held("identity", [P, P], F32)
+        make_identity(nc, identity[:])
+        for b in range(BLOCKS):
+            (nc.gpsimd if b % 2 == 0 else nc.vector).memset(windows[b][:], 0.0)
+
+        note_planes = [held("note_plane%d" % j, [P, U], F32) for j in range(PACK)]
+        query_raw = held("query_raw", [P, PACK, Q], F32)
+        query2_raw = held("query2_raw", [P, PACK, Q], F32)
+        key_words = held("key_words", [P, T], U32)
+        val_rows = [held("val_rows%d" % b, [P, T], F32) for b in range(BLOCKS)]
+        old_rows = [held("old_rows%d" % b, [P, M], F32) for b in range(BLOCKS)]
+
+        def load_vals(b):
+            nc.sync.dma_start(out=val_rows[b][:], in_=vals[b * P : (b + 1) * P, :])
+
+        def load_old(b):
+            nc.sync.dma_start(out=old_rows[b][:], in_=old[b * P : (b + 1) * P, :])
+
+        notes_by_place = notes.rearrange("(p j) u -> p j u", j=PACK)
+
+        def load_notes(j):
+            nc.sync.dma_start(out=note_planes[j][:], in_=notes_by_place[:, j, :])
+
+        nc.sync.dma_start(note_list[:], offs2)
+        load_notes(0)
+        nc.sync.dma_start(out=byte_rows[:], in_=keys_scales[0].bitcast(I32).rearrange("(g r) c -> r g c", r=4))
+        load_notes(1)
+        nc.sync.dma_start(token_list[:], offs)
+        load_notes(2)
+        nc.sync.dma_start(out=fade_cols[:], in_=fade.rearrange("o (p c) -> p (o c)", c=8))
+        load_notes(3)
+        nc.sync.dma_start(out=query2_raw[:], in_=query2.rearrange("(p j) q -> p j q", j=PACK))
+        nc.sync.dma_start(out=query_raw[:], in_=query.rearrange("(p j) q -> p j q", j=PACK))
+        nc.sync.dma_start(
+            out=key_words[:].bitcast(I32), in_=keys_words[0].rearrange("p n t -> p (n t)").bitcast(I32)
+        )
+        nc.sync.dma_start(out=factor[:], in_=slot_factor.rearrange("o (p t) -> p (o t)", t=PACK))
+        load_vals(0)
+        load_vals(1)
+        nc.sync.dma_start(place_list[:], offs3)
+        load_old(0)
+        load_vals(2)
+        load_old(1)
+        load_vals(3)
+        load_old(2)
+        load_old(3)
+
+        for g in range(4):
+            nc.vector.tensor_copy(out=key_bytes[32 * g : 32 * g + 4, :].bitcast(I32), in_=byte_rows[:, g, :])
+
+        notes_picked = held("notes_picked", [P, PACK, I], BF16)
+        for j in range(PACK):
+            if j % 2 == 0:
+                nc.scalar.activation(notes_picked[:, j, :], note_planes[j][:].indirect(note_list[:]), COPY)
+            else:
+                nc.vector.tensor_copy(notes_picked[:, j, :], note_planes[j][:].indirect(note_list[:]))
+        key_scales = held("key_scales", [P, PACK, P], U8, reuse="note_plane1")
+        nc.vector.tensor_copy(key_scales[:].rearrange("p t s -> p s t"), key_bytes[:].indirect(token_list[:]))
+        notes_grouped = held("notes_grouped", [P, I * PACK], BF16, reuse="key_bytes")
+        nc.vector.tensor_copy(
+            out=notes_grouped[:].rearrange("p (t a b j) -> p a t b j", t=PACK, b=2, j=PACK),
+            in_=notes_picked[:].rearrange("p j (a b t) -> p a t b j", b=2, t=PACK),
+        )
+        note_codes = held("note_codes", [P, I], U32)
+        note_scales = held("note_scales", [P, I], U8)
+        nc.vector.quantize_mx(out=note_codes[:].bitcast(FP8X4), scales=note_scales[:], in_=notes_grouped[:])
+
+        def quantised_query(name, raw):
+            grouped = held(name + "_grouped", [P, Q, PACK], BF16)
+            nc.scalar.copy(out=grouped[:], in_=raw[:].rearrange("p j q -> p q j"))
+            codes = held(name + "_codes", [P, Q], U32)
+            scales = held(name + "_scales", [P, Q], U8)
+            nc.vector.quantize_mx(
+                out=codes[:].bitcast(FP8X4), scales=scales[:], in_=grouped[:].rearrange("p q j -> p (q j)")
+            )
+            return codes, scales
+
+        query2_codes, query2_scales = quantised_query("query2", query2_raw)
+        query_codes, query_scales = quantised_query("query", query_raw)
+
+        fade_rows = held("fade_rows", [P, P, 8], F32, reuse="query_raw")
+        for k in range(2):
+            fade_bank = psum.tile([P, 4, P], F32, name="fade_bank%d" % k)
+            for c in range(4):
+                nc.tensor.transpose(
+                    fade_bank[:, c, :], fade_cols[:, 4 * k + c : 4 * k + c + 1].to_broadcast([P, P]), identity[:]
+                )
+            nc.scalar.copy(out=fade_rows[:, :, 4 * k : 4 * k + 4], in_=fade_bank[:].rearrange("p c s -> p s c"))
+
+        key_codes = held("key_codes", [P, PACK, P], U32, reuse="query_grouped")
+        nc.vector.tensor_copy(key_codes[:].rearrange("p t s -> p s t"), key_words[:].indirect(token_list[:]))
+
+        def gather_values(b):
+            picked = held("picked%d" % b, [P, I], BF16, reuse=("key_words", "gates0", "val_rows1", "val_rows2")[b])
+            if b == 0:
+                nc.vector.tensor_copy(picked[:], val_rows[b][:].indirect(token_list[:]))
+            else:
+                nc.scalar.activation(picked[:], val_rows[b][:].indirect(token_list[:]), COPY)
+            pairs = picked[:].bitcast(F32)
+            turned = psum.tile([P, 2, P], F32, name="turned", bufs=2)
+            for u in range(2):
+                nc.tensor.transpose(turned[:, u, :], pairs[:, u : I // 2 : 2], identity[:])
+            return turned
+
+        turned = gather_values(0)
+
+        score_banks = [psum.tile([P, PACK, HALF], F32, name="score_bank%d" % h) for h in range(2)]
+        for h in range(2):
+            cols = slice(h * HALF, (h + 1) * HALF)
+            for t in range(PACK):
+                nc.tensor.matmul_mx(
+                    out=score_banks[h][:, t, :],
+                    lhsT=note_codes[:, t * P : (t + 1) * P].bitcast(FP8X4),
+                    lhsT_scale=note_scales[:, t * P : (t + 1) * P],
+                    rhs=query2_codes[:, cols].bitcast(FP8X4),
+                    rhs_scale=query2_scales[:, cols],
+                    start=(t == 0),
+                    stop=False,
+                )
+        weight_codes = held("weight_codes", [P, Q], U32)
+        weight_scales = held("weight_scales", [P, Q], U8)
+        factor_spread = factor[:].rearrange("p (o t) -> p o t", o=1).to_broadcast([P, HALF, PACK])
+        for h in range(2):
+            cols = slice(h * HALF, (h + 1) * HALF)
+            for t in range(PACK):
+                nc.tensor.matmul_mx(
+                    out=score_banks[h][:, t, :],
+                    lhsT=key_codes[:, t, :].bitcast(FP8X4),
+                    lhsT_scale=key_scales[:, t, :],
+                    rhs=query_codes[:, cols].bitcast(FP8X4),
+                    rhs_scale=query_scales[:, cols],
+                    start=False,
+                    stop=(t == PACK - 1),
+                )
+            gates = held("gates%d" % h, [P, HALF, PACK], F32)
+            nc.scalar.activation(gates[:], score_banks[h][:].rearrange("p t q -> p q t"), SIGMOID)
+            weights = held("weights%d" % h, [P, HALF, PACK], BF16, reuse="val_rows0" if h == 0 else None)
+            nc.vector.tensor_tensor(weights[:], gates[:], factor_spread, MULT)
+            nc.vector.quantize_mx(
+                out=weight_codes[:, cols].bitcast(FP8X4),
+                scales=weight_scales[:, cols],
+                in_=weights[:].rearrange("p q t -> p (q t)"),
+            )
+
+        def multiply(b, turned):
+            grouped = held("val_grouped%d" % b, [P, P * PACK], BF16, reuse="old_rows%d" % (b - 1) if b > 0 else None)
+            nc.vector.tensor_copy(
+                out=grouped[:].bitcast(F32).rearrange("p (e u) -> p e u", u=2),
+                in_=turned[:].rearrange("p u e -> p e u"),
+            )
+            val_codes = held("val_codes%d" % b, [P, P], U32)
+            val_scales = held("val_scales%d" % b, [P, P], U8)
+            nc.vector.quantize_mx(out=val_codes[:].bitcast(FP8X4), scales=val_scales[:], in_=grouped[:])
+            read_bank = psum.tile([P, Q], F32, name="read_bank", bufs=2)
+            nc.tensor.matmul_mx(
+                out=read_bank[:],
+                lhsT=val_codes[:].bitcast(FP8X4),
+                lhsT_scale=val_scales[:],
+                rhs=weight_codes[:].bitcast(FP8X4),
+                rhs_scale=weight_scales[:],
+                start=True,
+                stop=True,
+            )
+            return read_bank
+
+        def scatter(b, read_bank):
+            read = held("read%d" % b, [P, Q], F32, reuse="val_rows%d" % min(b + 1, BLOCKS - 1))
+            nc.scalar.copy(out=read[:], in_=read_bank[:])
+            nc.scalar.activation(windows[b][:].indirect(place_list[:]), read[:], COPY)
+
+        def fade_old(b):
+            faded = held("faded%d" % b, [P, M], F32, reuse="val_grouped0" if b + 1 < BLOCKS else "old_rows2")
+            nc.vector.tensor_tensor(faded[:], old_rows[b][:], fade_rows[:].rearrange("p s c -> p (s c)"), MULT)
+            return faded
+
+        def finish(b, faded):
+            pieces = 2 if b == BLOCKS - 1 else 1
+            result = held("result%d" % b, [P, M], F32, reuse=("old_rows0", "old_rows1", "old_rows3", None)[b])
+            for k in range(pieces):
+                cols = slice(k * M // pieces, (k + 1) * M // pieces)
+                nc.vector.tensor_tensor(result[:, cols], faded[:, cols], windows[b][:, cols], ADD)
+                nc.sync.dma_start(out=out[b * P : (b + 1) * P, cols], in_=result[:, cols])
+
+        faded = None
+        for b in range(BLOCKS):
+            read_bank = multiply(b, turned)
+            if b + 1 < BLOCKS:
+                turned = gather_values(b + 1)
+            scatter(b, read_bank)
+            earlier = faded
+            if b == BLOCKS - 1:
+                faded = fade_old(b)
+            if b > 0:
+                finish(b - 1, earlier)
+            if b < BLOCKS - 1:
+                faded = fade_old(b)
+        finish(BLOCKS - 1, faded)

@@ -70,8 +70,8 @@ def tile_attend_twosources_written_lean_kernel(
             nc.sync.dma_start(out=note_planes[j][:], in_=notes_by_place[:, j, :])
 
         nc.sync.dma_start(note_list[:], offs2)
-        load_notes(0)
         nc.sync.dma_start(out=byte_rows[:], in_=keys_scales[0].bitcast(I32).rearrange("(g r) c -> r g c", r=4))
+        load_notes(0)
         load_notes(1)
         nc.sync.dma_start(token_list[:], offs)
         load_notes(2)
@@ -87,16 +87,16 @@ def tile_attend_twosources_written_lean_kernel(
         load_vals(1)
         nc.sync.dma_start(place_list[:], offs3)
         load_old(0)
-        load_vals(2)
         load_old(1)
-        load_vals(3)
+        load_vals(2)
         load_old(2)
+        load_vals(3)
         load_old(3)
 
         for g in range(4):
             nc.vector.tensor_copy(out=key_bytes[32 * g : 32 * g + 4, :].bitcast(I32), in_=byte_rows[:, g, :])
 
-        notes_picked = held("notes_picked", [P, PACK, I], BF16)
+        notes_picked = held("notes_picked", [P, PACK, I], BF16, reuse="byte_rows")
         for j in range(PACK):
             if j % 2 == 0:
                 nc.scalar.activation(notes_picked[:, j, :], note_planes[j][:].indirect(note_list[:]), COPY)
@@ -139,8 +139,8 @@ def tile_attend_twosources_written_lean_kernel(
         nc.vector.tensor_copy(key_codes[:].rearrange("p t s -> p s t"), key_words[:].indirect(token_list[:]))
 
         def gather_values(b):
-            picked = held("picked%d" % b, [P, I], BF16, reuse=("key_words", "gates0", "val_rows1", "val_rows2")[b])
-            if b == 0:
+            picked = held("picked%d" % b, [P, I], BF16, reuse=("key_words", "gates0", "val_rows1", "old_rows2")[b])
+            if b in (0, BLOCKS - 1):
                 nc.vector.tensor_copy(picked[:], val_rows[b][:].indirect(token_list[:]))
             else:
                 nc.scalar.activation(picked[:], val_rows[b][:].indirect(token_list[:]), COPY)
@@ -167,6 +167,7 @@ def tile_attend_twosources_written_lean_kernel(
                 )
         weight_codes = held("weight_codes", [P, Q], U32)
         weight_scales = held("weight_scales", [P, Q], U8)
+        weights = held("weights", [P, 2, HALF, PACK], BF16, reuse="val_rows0")
         factor_spread = factor[:].rearrange("p (o t) -> p o t", o=1).to_broadcast([P, HALF, PACK])
         for h in range(2):
             cols = slice(h * HALF, (h + 1) * HALF)
@@ -182,16 +183,15 @@ def tile_attend_twosources_written_lean_kernel(
                 )
             gates = held("gates%d" % h, [P, HALF, PACK], F32)
             nc.scalar.activation(gates[:], score_banks[h][:].rearrange("p t q -> p q t"), SIGMOID)
-            weights = held("weights%d" % h, [P, HALF, PACK], BF16, reuse="val_rows0" if h == 0 else None)
-            nc.vector.tensor_tensor(weights[:], gates[:], factor_spread, MULT)
+            nc.vector.tensor_tensor(weights[:, h], gates[:], factor_spread, MULT)
             nc.vector.quantize_mx(
                 out=weight_codes[:, cols].bitcast(FP8X4),
                 scales=weight_scales[:, cols],
-                in_=weights[:].rearrange("p q t -> p (q t)"),
+                in_=weights[:, h].rearrange("p q t -> p (q t)"),
             )
 
         def multiply(b, turned):
-            grouped = held("val_grouped%d" % b, [P, P * PACK], BF16, reuse="old_rows%d" % (b - 1) if b > 0 else None)
+            grouped = held("val_grouped%d" % b, [P, P * PACK], BF16, reuse=(None, "old_rows0", "old_rows2", "old_rows0")[b])
             nc.vector.tensor_copy(
                 out=grouped[:].bitcast(F32).rearrange("p (e u) -> p e u", u=2),
                 in_=turned[:].rearrange("p u e -> p e u"),
@@ -212,34 +212,33 @@ def tile_attend_twosources_written_lean_kernel(
             return read_bank
 
         def scatter(b, read_bank):
-            read = held("read%d" % b, [P, Q], F32, reuse="val_rows%d" % min(b + 1, BLOCKS - 1))
+            read = held("read%d" % b, [P, Q], F32, reuse=("val_rows1", "val_rows2", "val_rows2", "val_rows2")[b])
             nc.scalar.copy(out=read[:], in_=read_bank[:])
             nc.scalar.activation(windows[b][:].indirect(place_list[:]), read[:], COPY)
 
         def fade_old(b):
-            faded = held("faded%d" % b, [P, M], F32, reuse="val_grouped0" if b + 1 < BLOCKS else "old_rows2")
+            faded = held("faded%d" % b, [P, M], F32, reuse=("val_rows0", "old_rows0", "val_rows0", "old_rows0")[b])
             nc.vector.tensor_tensor(faded[:], old_rows[b][:], fade_rows[:].rearrange("p s c -> p (s c)"), MULT)
             return faded
 
         def finish(b, faded):
             pieces = 2 if b == BLOCKS - 1 else 1
-            result = held("result%d" % b, [P, M], F32, reuse=("old_rows0", "old_rows1", "old_rows3", None)[b])
+            result = held("result%d" % b, [P, M], F32, reuse=("old_rows1", "val_rows3", "old_rows3", None)[b])
             for k in range(pieces):
                 cols = slice(k * M // pieces, (k + 1) * M // pieces)
                 nc.vector.tensor_tensor(result[:, cols], faded[:, cols], windows[b][:, cols], ADD)
                 nc.sync.dma_start(out=out[b * P : (b + 1) * P, cols], in_=result[:, cols])
 
-        faded = None
+        faded = {}
         for b in range(BLOCKS):
             read_bank = multiply(b, turned)
             if b + 1 < BLOCKS:
                 turned = gather_values(b + 1)
             scatter(b, read_bank)
-            earlier = faded
-            if b == BLOCKS - 1:
-                faded = fade_old(b)
+            if b != 2:
+                faded[b] = fade_old(b)
             if b > 0:
-                finish(b - 1, earlier)
-            if b < BLOCKS - 1:
-                faded = fade_old(b)
-        finish(BLOCKS - 1, faded)
+                finish(b - 1, faded[b - 1])
+            if b == 1:
+                faded[2] = fade_old(2)
+        finish(BLOCKS - 1, faded[BLOCKS - 1])

@@ -44,12 +44,12 @@ def tile_attend_twosources_written_lean_kernel(
         nc.vector.memset(key_bytes[:].bitcast(I32), 0)
         factor = held("factor", [P, PACK], F32)
         fade_cols = held("fade_cols", [P, 8], F32)
-        byte_rows = held("byte_rows", [4, 4, T // 4], I32)
+        byte_rows = held("byte_rows", [P, 2, T // 4], I32)
         windows = [held("window%d" % b, [P, M], F32) for b in range(BLOCKS)]
         identity = held("identity", [P, P], F32)
         make_identity(nc, identity[:])
         for b in range(BLOCKS):
-            (nc.gpsimd if b % 2 == 0 else nc.vector).memset(windows[b][:], 0.0)
+            nc.vector.memset(windows[b][:], 0.0)
 
         note_planes = [held("note_plane%d" % j, [P, U], F32) for j in range(PACK)]
         query_raw = held("query_raw", [P, PACK, Q], F32)
@@ -70,7 +70,9 @@ def tile_attend_twosources_written_lean_kernel(
             nc.sync.dma_start(out=note_planes[j][:], in_=notes_by_place[:, j, :])
 
         nc.sync.dma_start(note_list[:], offs2)
-        nc.sync.dma_start(out=byte_rows[:], in_=keys_scales[0].bitcast(I32).rearrange("(g r) c -> r g c", r=4))
+        scale_words = keys_scales[0].bitcast(I32).rearrange("(g r) c -> r g c", r=4)
+        for k in range(2):
+            nc.sync.dma_start(out=byte_rows[64 * k : 64 * k + 4], in_=scale_words[:, 2 * k : 2 * k + 2, :])
         load_notes(0)
         load_notes(1)
         nc.sync.dma_start(token_list[:], offs)
@@ -89,12 +91,12 @@ def tile_attend_twosources_written_lean_kernel(
         load_old(0)
         load_old(1)
         load_vals(2)
-        load_old(2)
         load_vals(3)
+        load_old(2)
         load_old(3)
 
         for g in range(4):
-            nc.vector.tensor_copy(out=key_bytes[32 * g : 32 * g + 4, :].bitcast(I32), in_=byte_rows[:, g, :])
+            nc.vector.tensor_copy(out=key_bytes[32 * g : 32 * g + 4, :].bitcast(I32), in_=byte_rows[64 * (g // 2) : 64 * (g // 2) + 4, g % 2, :])
 
         notes_picked = held("notes_picked", [P, PACK, I], BF16, reuse="byte_rows")
         for j in range(PACK):
@@ -139,7 +141,7 @@ def tile_attend_twosources_written_lean_kernel(
         nc.vector.tensor_copy(key_codes[:].rearrange("p t s -> p s t"), key_words[:].indirect(token_list[:]))
 
         def gather_values(b):
-            picked = held("picked%d" % b, [P, I], BF16, reuse=("key_words", "gates0", "val_rows1", "old_rows2")[b])
+            picked = held("picked%d" % b, [P, I], BF16, reuse=("key_words", "gates0", "val_rows1", "val_rows0")[b])
             if b in (0, BLOCKS - 1):
                 nc.vector.tensor_copy(picked[:], val_rows[b][:].indirect(token_list[:]))
             else:
@@ -191,7 +193,7 @@ def tile_attend_twosources_written_lean_kernel(
             )
 
         def multiply(b, turned):
-            grouped = held("val_grouped%d" % b, [P, P * PACK], BF16, reuse=(None, "old_rows0", "old_rows2", "old_rows0")[b])
+            grouped = held("val_grouped%d" % b, [P, P * PACK], BF16, reuse=(None, "old_rows0", "val_rows3", "val_rows3")[b])
             nc.vector.tensor_copy(
                 out=grouped[:].bitcast(F32).rearrange("p (e u) -> p e u", u=2),
                 in_=turned[:].rearrange("p u e -> p e u"),
@@ -217,28 +219,30 @@ def tile_attend_twosources_written_lean_kernel(
             nc.scalar.activation(windows[b][:].indirect(place_list[:]), read[:], COPY)
 
         def fade_old(b):
-            faded = held("faded%d" % b, [P, M], F32, reuse=("val_rows0", "old_rows0", "val_rows0", "old_rows0")[b])
+            faded = held("faded%d" % b, [P, M], F32, reuse=("val_rows0", "old_rows0", "val_rows3", "val_rows3")[b])
             nc.vector.tensor_tensor(faded[:], old_rows[b][:], fade_rows[:].rearrange("p s c -> p (s c)"), MULT)
             return faded
 
         def finish(b, faded):
             pieces = 2 if b == BLOCKS - 1 else 1
-            result = held("result%d" % b, [P, M], F32, reuse=("old_rows1", "val_rows3", "old_rows3", None)[b])
+            result = held("result%d" % b, [P, M], F32, reuse=("old_rows1", "val_codes2", None, None)[b])
             for k in range(pieces):
                 cols = slice(k * M // pieces, (k + 1) * M // pieces)
                 nc.vector.tensor_tensor(result[:, cols], faded[:, cols], windows[b][:, cols], ADD)
                 nc.sync.dma_start(out=out[b * P : (b + 1) * P, cols], in_=result[:, cols])
 
-        faded = {}
-        for b in range(BLOCKS):
-            read_bank = multiply(b, turned)
-            if b + 1 < BLOCKS:
-                turned = gather_values(b + 1)
-            scatter(b, read_bank)
-            if b != 2:
-                faded[b] = fade_old(b)
-            if b > 0:
-                finish(b - 1, faded[b - 1])
-            if b == 1:
-                faded[2] = fade_old(2)
-        finish(BLOCKS - 1, faded[BLOCKS - 1])
+        read_bank = multiply(0, turned)
+        turned = gather_values(1)
+        scatter(0, read_bank)
+        faded0 = fade_old(0)
+        read_bank = multiply(1, turned)
+        turned = gather_values(2)
+        scatter(1, read_bank)
+        faded1 = fade_old(1)
+        finish(0, faded0)
+        turned_last = gather_values(3)
+        scatter(2, multiply(2, turned))
+        scatter(3, multiply(3, turned_last))
+        finish(1, faded1)
+        for b in (2, 3):
+            finish(b, fade_old(b))

@@ -43,7 +43,7 @@ def tile_attend_twosources_written_lean_kernel(
         key_bytes = held("key_bytes", [P, T], U8)
         nc.vector.memset(key_bytes[:].bitcast(I32), 0)
         factor = held("factor", [P, PACK], F32)
-        fade_cols = held("fade_cols", [P, 8], F32)
+        fade_cols = held("fade_cols", [P, 2, 4], F32)
         byte_rows = held("byte_rows", [P, 2, T // 4], I32)
         windows = [held("window%d" % b, [P, M], F32) for b in range(BLOCKS)]
         identity = held("identity", [P, P], F32)
@@ -77,7 +77,7 @@ def tile_attend_twosources_written_lean_kernel(
         load_notes(1)
         nc.sync.dma_start(token_list[:], offs)
         load_notes(2)
-        nc.sync.dma_start(out=fade_cols[:], in_=fade.rearrange("o (p c) -> p (o c)", c=8))
+        nc.sync.dma_start(out=fade_cols[:], in_=fade.rearrange("o (k p c) -> p (o k) c", k=2, c=4))
         load_notes(3)
         nc.sync.dma_start(out=query2_raw[:], in_=query2.rearrange("(p j) q -> p j q", j=PACK))
         nc.sync.dma_start(out=query_raw[:], in_=query.rearrange("(p j) q -> p j q", j=PACK))
@@ -128,14 +128,10 @@ def tile_attend_twosources_written_lean_kernel(
         query2_codes, query2_scales = quantised_query("query2", query2_raw)
         query_codes, query_scales = quantised_query("query", query_raw)
 
-        fade_rows = held("fade_rows", [P, P, 8], F32, reuse="query_raw")
+        fade_banks = [psum.tile([P, 4, P], F32, name="fade_bank%d" % k) for k in range(2)]
         for k in range(2):
-            fade_bank = psum.tile([P, 4, P], F32, name="fade_bank%d" % k)
             for c in range(4):
-                nc.tensor.transpose(
-                    fade_bank[:, c, :], fade_cols[:, 4 * k + c : 4 * k + c + 1].to_broadcast([P, P]), identity[:]
-                )
-            nc.scalar.copy(out=fade_rows[:, :, 4 * k : 4 * k + 4], in_=fade_bank[:].rearrange("p c s -> p s c"))
+                nc.tensor.transpose(fade_banks[k][:, c, :], fade_cols[:, k, c : c + 1].to_broadcast([P, P]), identity[:])
 
         key_codes = held("key_codes", [P, PACK, P], U32, reuse="query_grouped")
         nc.vector.tensor_copy(key_codes[:].rearrange("p t s -> p s t"), key_words[:].indirect(token_list[:]))
@@ -214,21 +210,31 @@ def tile_attend_twosources_written_lean_kernel(
             return read_bank
 
         def scatter(b, read_bank):
-            read = held("read%d" % b, [P, Q], F32, reuse=("val_rows1", "val_rows2", "val_rows2", "val_rows2")[b])
-            nc.scalar.copy(out=read[:], in_=read_bank[:])
+            read = held("read%d" % b, [P, Q], F32, reuse=("val_rows1", "val_rows2", "val_rows2", None)[b])
+            if b == BLOCKS - 1:
+                nc.vector.tensor_copy(out=read[:], in_=read_bank[:])
+            else:
+                nc.scalar.copy(out=read[:], in_=read_bank[:])
             nc.scalar.activation(windows[b][:].indirect(place_list[:]), read[:], COPY)
 
         def fade_old(b):
-            faded = held("faded%d" % b, [P, M], F32, reuse=("val_rows0", "old_rows0", "val_rows3", "val_rows3")[b])
-            nc.vector.tensor_tensor(faded[:], old_rows[b][:], fade_rows[:].rearrange("p s c -> p (s c)"), MULT)
+            faded = held("faded%d" % b, [P, M], F32, reuse=("val_rows0", "old_rows0", "val_codes2", "val_codes3")[b])
+            for k in range(2):
+                cols = slice(k * M // 2, (k + 1) * M // 2)
+                nc.vector.tensor_tensor(
+                    faded[:, cols].rearrange("p (s c) -> p s c", c=4),
+                    old_rows[b][:, cols].rearrange("p (s c) -> p s c", c=4),
+                    fade_banks[k][:].rearrange("p c s -> p s c"),
+                    MULT,
+                )
             return faded
 
         def finish(b, faded):
             pieces = 2 if b == BLOCKS - 1 else 1
-            result = held("result%d" % b, [P, M], F32, reuse=("old_rows1", "val_codes2", None, None)[b])
+            result = held("result%d" % b, [P, M], F32, reuse=("old_rows1", "val_rows3", None, None)[b])
             for k in range(pieces):
                 cols = slice(k * M // pieces, (k + 1) * M // pieces)
-                nc.vector.tensor_tensor(result[:, cols], faded[:, cols], windows[b][:, cols], ADD)
+                (nc.gpsimd if b == 1 else nc.vector).tensor_tensor(result[:, cols], faded[:, cols], windows[b][:, cols], ADD)
                 nc.sync.dma_start(out=out[b * P : (b + 1) * P, cols], in_=result[:, cols])
 
         read_bank = multiply(0, turned)
@@ -244,5 +250,7 @@ def tile_attend_twosources_written_lean_kernel(
         scatter(2, multiply(2, turned))
         scatter(3, multiply(3, turned_last))
         finish(1, faded1)
-        for b in (2, 3):
-            finish(b, fade_old(b))
+        faded2 = fade_old(2)
+        faded3 = fade_old(3)
+        finish(2, faded2)
+        finish(3, faded3)

from contextlib import ExitStack

import concourse.mybir as mybir
from concourse.masks import make_identity

D, T, I, Q, E, U, M = 512, 2048, 512, 256, 512, 1024, 1024
FLOPS = 2 * (2 * D * Q * I + I * E * Q)

F32 = mybir.dt.float32
BF16 = mybir.dt.bfloat16
I32 = mybir.dt.int32
U32 = mybir.dt.uint32
U16 = mybir.dt.uint16
U8 = mybir.dt.uint8
FP8X4 = mybir.dt.float8_e4m3fn_x4
COPY = mybir.ActivationFunctionType.Copy
SIGMOID = mybir.ActivationFunctionType.Sigmoid
MULT = mybir.AluOpType.mult
ADD = mybir.AluOpType.add

P = 128
PACK = 4
BLOCKS = E // P
HALF = Q // 2


def tile_attend_twosources_written_lean_kernel(
    tc, query, query2, keys_words, keys_scales, notes, slot_factor, vals, old, fade, offs, offs2, offs3, out
):
    nc = tc.nc
    with ExitStack() as ctx:
        lists = ctx.enter_context(tc.tile_pool(name="lists", bufs=1))
        keep = ctx.enter_context(tc.tile_pool(name="keep", bufs=1))
        psum = ctx.enter_context(tc.psum_pool(name="psum", bufs=1))

        token_list = lists.tile([P, I // 16], U16, name="token_list")
        note_list = lists.tile([P, I // 16], U16, name="note_list")
        place_list = lists.tile([P, Q // 16], U16, name="place_list")

        def held(name, shape, dtype, reuse=None):
            return keep.tile(shape, dtype, name=name, tag=reuse or name, align_bytes=64)

        key_bytes = held("key_bytes", [P, T], U8)
        nc.vector.memset(key_bytes[:].bitcast(I32), 0)
        factor = held("factor", [P, PACK], F32)
        fade_cols = held("fade_cols", [P, 2, 4], F32)
        byte_rows = held("byte_rows", [P, 2, T // 4], I32)
        windows = [held("window%d" % b, [P, M], F32) for b in range(BLOCKS)]
        identity = held("identity", [P, P], F32)
        make_identity(nc, identity[:])
        for b in range(BLOCKS):
            nc.vector.memset(windows[b][:], 0.0)

        note_planes = [held("note_plane%d" % j, [P, U], F32) for j in range(PACK)]
        query_raw = held("query_raw", [P, PACK, Q], F32)
        query2_raw = held("query2_raw", [P, PACK, Q], F32)
        key_words = held("key_words", [P, T], U32)
        val_rows = [held("val_rows%d" % b, [P, T], F32) for b in range(BLOCKS)]
        old_rows = [held("old_rows%d" % b, [P, M], F32) for b in range(BLOCKS)]

        def load_vals(b):
            nc.sync.dma_start(out=val_rows[b][:], in_=vals[b * P : (b + 1) * P, :])

        def load_old(b):
            nc.sync.dma_start(out=old_rows[b][:], in_=old[b * P : (b + 1) * P, :])

        notes_by_place = notes.rearrange("(p j) u -> p j u", j=PACK)

        def load_notes(j):
            nc.sync.dma_start(out=note_planes[j][:], in_=notes_by_place[:, j, :])

        nc.sync.dma_start(note_list[:], offs2)
        scale_words = keys_scales[0].bitcast(I32).rearrange("(g r) c -> r g c", r=4)
        for k in range(2):
            nc.sync.dma_start(out=byte_rows[64 * k : 64 * k + 4], in_=scale_words[:, 2 * k : 2 * k + 2, :])
        load_notes(0)
        load_notes(1)
        nc.sync.dma_start(token_list[:], offs)
        load_notes(2)
        nc.sync.dma_start(out=fade_cols[:], in_=fade.rearrange("o (k p c) -> p (o k) c", k=2, c=4))
        load_notes(3)
        nc.sync.dma_start(out=query2_raw[:], in_=query2.rearrange("(p j) q -> p j q", j=PACK))
        nc.sync.dma_start(out=query_raw[:], in_=query.rearrange("(p j) q -> p j q", j=PACK))
        nc.sync.dma_start(
            out=key_words[:].bitcast(I32), in_=keys_words[0].rearrange("p n t -> p (n t)").bitcast(I32)
        )
        nc.sync.dma_start(out=factor[:], in_=slot_factor.rearrange("o (p t) -> p (o t)", t=PACK))
        load_vals(0)
        load_vals(1)
        nc.sync.dma_start(place_list[:], offs3)
        load_old(0)
        load_old(1)
        load_vals(2)
        load_vals(3)
        load_old(2)
        load_old(3)

        for g in range(4):
            nc.vector.tensor_copy(out=key_bytes[32 * g : 32 * g + 4, :].bitcast(I32), in_=byte_rows[64 * (g // 2) : 64 * (g // 2) + 4, g % 2, :])

        notes_picked = held("notes_picked", [P, PACK, I], BF16, reuse="byte_rows")
        for j in range(PACK):
            if j % 2 == 0:
                nc.scalar.activation(notes_picked[:, j, :], note_planes[j][:].indirect(note_list[:]), COPY)
            else:
                nc.vector.tensor_copy(notes_picked[:, j, :], note_planes[j][:].indirect(note_list[:]))
        key_scales = held("key_scales", [P, PACK, P], U8, reuse="note_plane1")
        nc.vector.tensor_copy(key_scales[:].rearrange("p t s -> p s t"), key_bytes[:].indirect(token_list[:]))
        notes_grouped = held("notes_grouped", [P, I * PACK], BF16, reuse="key_bytes")
        nc.vector.tensor_copy(
            out=notes_grouped[:].rearrange("p (t a b j) -> p a t b j", t=PACK, b=2, j=PACK),
            in_=notes_picked[:].rearrange("p j (a b t) -> p a t b j", b=2, t=PACK),
        )
        note_codes = held("note_codes", [P, I], U32)
        note_scales = held("note_scales", [P, I], U8)
        nc.vector.quantize_mx(out=note_codes[:].bitcast(FP8X4), scales=note_scales[:], in_=notes_grouped[:])

        def quantised_query(name, raw):
            grouped = held(name + "_grouped", [P, Q, PACK], BF16)
            nc.scalar.copy(out=grouped[:], in_=raw[:].rearrange("p j q -> p q j"))
            codes = held(name + "_codes", [P, Q], U32)
            scales = held(name + "_scales", [P, Q], U8)
            nc.vector.quantize_mx(
                out=codes[:].bitcast(FP8X4), scales=scales[:], in_=grouped[:].rearrange("p q j -> p (q j)")
            )
            return codes, scales

        query2_codes, query2_scales = quantised_query("query2", query2_raw)
        query_codes, query_scales = quantised_query("query", query_raw)

        fade_banks = [psum.tile([P, 4, P], F32, name="fade_bank%d" % k) for k in range(2)]
        for k in range(2):
            for c in range(4):
                nc.tensor.transpose(fade_banks[k][:, c, :], fade_cols[:, k, c : c + 1].to_broadcast([P, P]), identity[:])

        key_codes = held("key_codes", [P, PACK, P], U32, reuse="query_grouped")
        nc.vector.tensor_copy(key_codes[:].rearrange("p t s -> p s t"), key_words[:].indirect(token_list[:]))

        def gather_values(b):
            picked = held("picked%d" % b, [P, I], BF16, reuse=("key_words", "gates0", "val_rows1", "val_rows0")[b])
            if b in (0, BLOCKS - 1):
                nc.vector.tensor_copy(picked[:], val_rows[b][:].indirect(token_list[:]))
            else:
                nc.scalar.activation(picked[:], val_rows[b][:].indirect(token_list[:]), COPY)
            pairs = picked[:].bitcast(F32)
            turned = psum.tile([P, 2, P], F32, name="turned", bufs=2)
            for u in range(2):
                nc.tensor.transpose(turned[:, u, :], pairs[:, u : I // 2 : 2], identity[:])
            return turned

        turned = gather_values(0)

        score_banks = [psum.tile([P, PACK, HALF], F32, name="score_bank%d" % h) for h in range(2)]
        for h in range(2):
            cols = slice(h * HALF, (h + 1) * HALF)
            for t in range(PACK):
                nc.tensor.matmul_mx(
                    out=score_banks[h][:, t, :],
                    lhsT=note_codes[:, t * P : (t + 1) * P].bitcast(FP8X4),
                    lhsT_scale=note_scales[:, t * P : (t + 1) * P],
                    rhs=query2_codes[:, cols].bitcast(FP8X4),
                    rhs_scale=query2_scales[:, cols],
                    start=(t == 0),
                    stop=False,
                )
        weight_codes = held("weight_codes", [P, Q], U32)
        weight_scales = held("weight_scales", [P, Q], U8)
        weights = held("weights", [P, 2, HALF, PACK], BF16, reuse="val_rows0")
        factor_spread = factor[:].rearrange("p (o t) -> p o t", o=1).to_broadcast([P, HALF, PACK])
        for h in range(2):
            cols = slice(h * HALF, (h + 1) * HALF)
            for t in range(PACK):
                nc.tensor.matmul_mx(
                    out=score_banks[h][:, t, :],
                    lhsT=key_codes[:, t, :].bitcast(FP8X4),
                    lhsT_scale=key_scales[:, t, :],
                    rhs=query_codes[:, cols].bitcast(FP8X4),
                    rhs_scale=query_scales[:, cols],
                    start=False,
                    stop=(t == PACK - 1),
                )
            gates = held("gates%d" % h, [P, HALF, PACK], F32)
            nc.scalar.activation(gates[:], score_banks[h][:].rearrange("p t q -> p q t"), SIGMOID)
            nc.vector.tensor_tensor(weights[:, h], gates[:], factor_spread, MULT)
            nc.vector.quantize_mx(
                out=weight_codes[:, cols].bitcast(FP8X4),
                scales=weight_scales[:, cols],
                in_=weights[:, h].rearrange("p q t -> p (q t)"),
            )

        def multiply(b, turned):
            grouped = held("val_grouped%d" % b, [P, P * PACK], BF16, reuse=(None, "old_rows0", "val_rows3", "val_rows3")[b])
            nc.vector.tensor_copy(
                out=grouped[:].bitcast(F32).rearrange("p (e u) -> p e u", u=2),
                in_=turned[:].rearrange("p u e -> p e u"),
            )
            val_codes = held("val_codes%d" % b, [P, P], U32)
            val_scales = held("val_scales%d" % b, [P, P], U8)
            nc.vector.quantize_mx(out=val_codes[:].bitcast(FP8X4), scales=val_scales[:], in_=grouped[:])
            read_bank = psum.tile([P, Q], F32, name="read_bank", bufs=2)
            nc.tensor.matmul_mx(
                out=read_bank[:],
                lhsT=val_codes[:].bitcast(FP8X4),
                lhsT_scale=val_scales[:],
                rhs=weight_codes[:].bitcast(FP8X4),
                rhs_scale=weight_scales[:],
                start=True,
                stop=True,
            )
            return read_bank

        def scatter(b, read_bank):
            read = held("read%d" % b, [P, Q], F32, reuse=("val_rows1", "val_rows2", "val_rows2", None)[b])
            if b == BLOCKS - 1:
                nc.vector.tensor_copy(out=read[:], in_=read_bank[:])
            else:
                nc.scalar.copy(out=read[:], in_=read_bank[:])
            nc.scalar.activation(windows[b][:].indirect(place_list[:]), read[:], COPY)

        def fade_old(b):
            faded = held("faded%d" % b, [P, M], F32, reuse=("val_rows0", "old_rows0", "val_codes2", "val_codes3")[b])
            for k in range(2):
                cols = slice(k * M // 2, (k + 1) * M // 2)
                nc.vector.tensor_tensor(
                    faded[:, cols].rearrange("p (s c) -> p s c", c=4),
                    old_rows[b][:, cols].rearrange("p (s c) -> p s c", c=4),
                    fade_banks[k][:].rearrange("p c s -> p s c"),
                    MULT,
                )
            return faded

        def finish(b, faded):
            pieces = 2 if b == BLOCKS - 1 else 1
            result = held("result%d" % b, [P, M], F32, reuse=("old_rows1", "val_rows3", None, None)[b])
            for k in range(pieces):
                cols = slice(k * M // pieces, (k + 1) * M // pieces)
                (nc.gpsimd if b == 1 else nc.vector).tensor_tensor(result[:, cols], faded[:, cols], windows[b][:, cols], ADD)
                nc.sync.dma_start(out=out[b * P : (b + 1) * P, cols], in_=result[:, cols])

        read_bank = multiply(0, turned)
        turned = gather_values(1)
        scatter(0, read_bank)
        faded0 = fade_old(0)
        read_bank = multiply(1, turned)
        turned = gather_values(2)
        scatter(1, read_bank)
        faded1 = fade_old(1)
        finish(0, faded0)
        turned_last = gather_values(3)
        scatter(2, multiply(2, turned))
        scatter(3, multiply(3, turned_last))
        finish(1, faded1)
        faded2 = fade_old(2)
        faded3 = fade_old(3)
        finish(2, faded2)
        finish(3, faded3)
